import numpy as np, ml_dtypes
CORES = [23,119,17,113]
N = 4
import mx_ref
BF = ml_dtypes.bfloat16
def tile(rs):
    return np.stack(rs, axis=2).reshape(128, -1).astype(BF)
def pick(q, e):
    c = np.concatenate([q[0].reshape(128, -1, 4), np.zeros((128, 1, 4), np.uint8)], axis=1); s = np.concatenate([q[1], np.ones((16, 1), np.uint8)], axis=1)
    return (np.ascontiguousarray(c[:, e].reshape(128, -1)), np.ascontiguousarray(s[:, e]))
def join(*qs):
    return (np.concatenate([q[0] for q in qs], axis=1), np.concatenate([q[1] for q in qs], axis=1))
def put(q, e, v):
    c, s = q[0].reshape(128, -1, 4).copy(), q[1].copy(); c[:, e] = v[0].reshape(128, -1, 4); s[:, e] = v[1]
    return (c.reshape(128, -1), s)
def pk(c, s):
    return (np.ascontiguousarray(c), mx_ref.live(s))
def emit(q):
    return q[0], q[1]
def packed(v, rng):
    q = [mx_ref.quantize(np.ascontiguousarray(v[r])) for r in range(N)]
    return np.stack([a for a, b in q]), np.stack([mx_ref.plane(b, rng) for a, b in q])
def values_of_codes():
    e, c = np.zeros((128, 128, 4), np.float32), np.zeros((128, 2, 4), np.uint8)
    e[np.arange(128), np.arange(128), 0] = 1
    c[:127, :, 0] = np.arange(256).reshape(2, 128).T[:127]
    return mx_ref.matmul(mx_ref.quantize(e.reshape(128, 512).astype(BF)), (c.reshape(128, 8), np.full((16, 2), 127, np.uint8))).T.reshape(-1).astype(np.float64)
CODE_VALUE, SCALE_VALUE = values_of_codes(), 2.0 ** (np.arange(256) - 127.0)
def decode(q):
    return (CODE_VALUE[q[0]].reshape(16, 8, -1, 4) * SCALE_VALUE[q[1]][:, None, :, None] + 0.0).reshape(128, -1).astype(np.float32)
def f(rng, *shape):
    return mx_ref.flush((rng.standard_normal(shape, dtype=np.float32) * np.exp2(rng.integers(-2, 3, shape[:-1] + (1,)))).astype(BF))
def wide(rng, *shape, cols=0):
    v = rng.standard_normal(shape, dtype=np.float32) * np.exp2(rng.integers(-12, 13, shape)).astype(np.float32)
    if cols: v *= np.repeat(np.exp2(rng.integers(-cols, cols + 1, shape[:-2] + (1, shape[-1] // 4))) * (rng.random(shape[:-2] + (1, shape[-1] // 4)) > 0.0625), 4, axis=-1).astype(np.float32)
    return mx_ref.flush(v.astype(BF))
C, E, K = 384, 6, 64
STEP = [1, 2, 3]
def numbers_of(rng):
    return {"x": np.array(f(rng, N, 128, 4 * C)), "u": np.array(f(rng, N, 128, 512)), "v": np.array(f(rng, N, 128, 512))}
def layers(rng):
    return np.array(f(rng, N, 128, 2048)).reshape(N, 8, 16, 4, 8, 16, 4)
def held(w, parts):
    for i in parts:
        w[:, :, i] = 0
        w[:, :, :, :, :, i] = 0
    for i in parts:
        for g in range(8):
            for b in range(4): w[:, g, i, b, g, i, b] = 64
    return w
def weights(rng, w):
    c, p = packed(np.ascontiguousarray(w).reshape(N, 128, 2048), rng)
    return {"wc": c, "ws": p}
def setup_inputs(rng):
    return {**numbers_of(rng), **weights(rng, layers(rng))}
def setup_inputs_ties(rng):
    d = numbers_of(rng)
    x = d["x"].astype(np.float32).reshape(N, 8, 16, C, 4)
    x[:, :, 0] = 0
    x[:, :, 0, :, 0] = rng.integers(0, 4, (N, 8, C))
    z = (N, 8, 8, C, 4)
    x[:, :, 8:] = (2 * rng.integers(0, 8, z) + 1) * (2.0 * rng.integers(0, 2, z) - 1.0) * np.exp2(-1.0 * rng.integers(12, 19, z))
    x[:, :, 8, :, 0] = 1.96875
    u = d["u"].reshape(N, 128, 128, 4)
    u[:, :, ::16] = 0
    o = rng.permutation(N)
    for r in range(N):
        for h in range(0, 128, 16): u[r, h, h, 0] = 0.0 if r == o[0] else -1.0 if r == o[1] else 1.0
    w = layers(rng)
    w[:, :, 8, :, :, :, 0] = 0
    for r in o[3::2]:
        k = (r + STEP[0]) % N
        w[k, :, :, :, :, 8:] = 0
        for g in range(8):
            x[r, g, 8, :, 0] = 1.125
            x[r, g, 9, :, 0] = (3 + 2 * (g % 2)) * 2.0 ** (-14 - g // 2)
            u[r, 16 * g + 9, 16 * g, 0] = 1.0
            w[k, g, 8, 0, g, 8, 0] = 56
            w[k, g, 9, 0, g, 9, 0] = 32
    return {"x": x.reshape(N, 128, 4 * C).astype(BF), "u": u.reshape(N, 128, 512), "v": d["v"], **weights(rng, held(w, [0]))}
def setup_inputs_near(rng):
    d = numbers_of(rng)
    x = d["x"].astype(np.float32).reshape(N, 8, 16, C, 4)
    x[:, :, 0] = 0
    x[:, :, 8:] = 0
    x[:, :, 0, :, 0] = rng.integers(0, 2, (N, 8, C)) * 2.0 - 1.0
    s = rng.integers(0, 16, (N, 8, C))
    x[:, :, 8] = ((s[:, :, :, None] >> np.arange(4)) & 1) * np.exp2(np.arange(4) - 23.0)
    x[:, :, 11, :, 0] = 2.0 ** -10
    u = d["u"].reshape(N, 128, 128, 4)
    u[:, :, ::16] = 0
    o = rng.permutation(N) % 4
    for r in range(N):
        k = 1.0 if o[r] == 0 else 2.0 ** -30
        if o[r] == 2:
            x[r, :, 0] = 0
            x[r, :, 11] = 0
            for g in rng.permutation(8)[:4]: x[r, g, 0, rng.integers(C), 0] = 2.0 ** 16 * rng.choice([-1.0, 1.0])
        if o[r] == 3:
            x[r, :, 0] = 0
            x[r, :, 8:] = 0
            x[r, :, 10, :, 0] = rng.integers(-4, 5, (8, C)) * 2.0 ** -30
        for h in range(0, 128, 16):
            if o[r] < 2:
                u[r, h, h, 0] = k
                u[r, h + 11, h, 0] = k
            if o[r] == 2: u[r, h, h, 0] = 1.0
            if o[r] < 3: u[r, h + 8, h] = k
            else: u[r, h + 10, h, 0] = k
    w = held(layers(rng), [0, 8, 9, 10, 11, 12, 13, 14, 15])
    return {"x": x.reshape(N, 128, 4 * C).astype(BF), "u": u.reshape(N, 128, 512), "v": d["v"], **weights(rng, w)}
def setup_inputs_huge(rng):
    d = numbers_of(rng)
    o = rng.permutation(N)
    x = (0.8 + 0.2 * rng.random((N, 8, 16, C, 4))) * 1.4 * 2.0 ** 25
    c = rng.integers(0, 2, (N, 1, 1, C, 1)) * 2.0 - 1.0
    c[o < N // 2] = -1.0
    u = d["u"].reshape(N, 128, 128, 4)
    for r in range(N):
        a = 2.0 ** 30 * (1.0 - 0.1 * rng.random((128, 8, 4))) * (rng.permutation(8) % 2 * 2.0 - 1.0)[None, :, None]
        u[r, :, ::16] = a.astype(np.float32).astype(BF)
    w = np.zeros((N, 128, 4, 128, 4), np.float32)
    i = np.arange(128)
    for b in range(4): w[:, i, b, i, b] = 8
    return {"x": (x * c).astype(np.float32).reshape(N, 128, 4 * C).astype(BF), "u": u.reshape(N, 128, 512), "v": d["v"], **weights(rng, w.astype(BF))}
def setup_inputs_ends(rng):
    d = numbers_of(rng)
    e = rng.permutation(N)
    a = np.float32(1.9375 * 2.0 ** 25)
    x = d["x"].astype(np.float32).reshape(N, 8, 16, C, 4)
    u = d["u"].reshape(N, 128, 128, 4)
    u[:, :, ::16] = (2.0 ** 30 * rng.choice([-1.0, 1.0], (N, 1, 8, 1))).astype(np.float32).astype(BF)
    for r in range(N):
        if r == e[0]: x[r] = -a
        elif r == e[1]: x[r] = a * rng.choice([-1.0, 1.0], (1, 1, C, 1))
        elif r == e[2]: x[r] = a * rng.choice([-1.0, 1.0], (8, 16, C, 4))
        elif r == e[3]:
            x[r, :, 8:] = 0
            x[r, :, 8, :, 0] = rng.integers(-1, 2, (8, C)) * 2.0 ** -30
            u[r, :, ::16] = 0
            for h in range(0, 128, 16): u[r, h + 8, h, 0] = 2.0 ** -30
        else: x[r] = -a * rng.choice([0.5, 1.0], (8, 16, C, 4))
    w = layers(rng).astype(np.float32) * np.float32(2.0 ** -10)
    w[:, :, :, :, :, 8:] = 0
    d["v"] = (np.where(d["v"] < 0, -1.0, 1.0) * np.where(rng.permutation(N) % 2, 2.0 ** -30, 2.0 ** 30)[:, None, None]).astype(np.float32).astype(BF)
    return {"x": x.reshape(N, 128, 4 * C).astype(BF), "u": u.reshape(N, 128, 512), "v": d["v"], **weights(rng, mx_ref.flush(w.astype(BF)))}
def setup_inputs_spread(rng):
    d = setup_inputs(rng)
    d["x"] = np.clip(wide(rng, N, 128, 4 * C, cols=3).astype(np.float32), -65536.0, 65536.0).astype(BF)
    return d
def check_inputs(d):
    b = []
    for k in ("x", "u", "v"):
        a = np.abs(d[k].astype(np.float32))
        if not (np.isfinite(a).all() and ((a == 0) | (a >= 2.0 ** -30) & (a <= 2.0 ** 30)).all()): b.append("a value of " + k)
    none, least, most = [emit(mx_ref.quantize(np.full((128, 16), k, np.float32).astype(BF)))[1][0, 0] for k in (0.0, 2.0 ** -30, 2.0 ** 30)]
    top = 0.0
    for r in range(N):
        if ((d["wc"][r] == 0x7F) | (d["wc"][r] == 0xFF)).any(): b.append("wc: a code that is no number")
        s = mx_ref.live(d["ws"][r])
        if ((s != none) & ((s < least) | (s > most))).any(): b.append("ws: a scale out of range")
        w = np.abs(decode(pk(d["wc"][r], d["ws"][r])).astype(np.float64)).reshape(128, 512, 4)
        top = max(top, float(np.max(np.sum(w, axis=(0, 2)))))
    g = min(2.5 + 0.02 * top, 1e60)
    if not g * g * g * float(np.max(np.abs(d["x"].astype(np.float32)))) <= 2.0 ** 30: b.append("x and W: the bound of what they make")
    return b
def reference(x, u, v, wc, ws):
    qu = [mx_ref.quantize(u[r]) for r in range(N)]
    lay = [[pick(pk(wc[r], ws[r]), np.arange(128 * b, 128 * b + 128)) for b in range(4)] for r in range(N)]
    now = [x[r] for r in range(N)]
    for t in range(len(STEP)):
        first = np.arange(t % 2, 8, 2)
        second = (first + 1) % 8
        made = []
        for r in range(N):
            q = mx_ref.quantize(now[r])
            s = mx_ref.matmul(qu[r], q)[::16] + np.float32(0.0)
            o = np.argsort(-s, axis=1, kind="stable")[:, None, :, None]
            a = np.take_along_axis(decode(q).reshape(8, 16, C, 4), o, axis=2).reshape(8, 16, K, E, 4)
            m = np.max(a, axis=3)
            qm = mx_ref.quantize(np.ascontiguousarray(m.reshape(128, 4 * K)).astype(BF))
            back = mx_ref.quantize(tile([mx_ref.matmul(w, qm) * np.float32(0.015625) for w in lay[(r + STEP[t]) % N]]))
            p = decode(back).reshape(8, 16, K, 4)
            c = mx_ref.matmul(qu[r], back)[::16] + np.float32(0.0)
            swap = c[first] < c[second]
            source = np.zeros((8, K), np.int64)
            source[first] = np.where(swap, second[:, None], first[:, None])
            source[second] = np.where(swap, first[:, None], second[:, None])
            away = (a - m[:, :, :, None]).transpose(0, 2, 1, 3, 4)[source, np.arange(K)].transpose(0, 2, 1, 3, 4)
            new = np.zeros((8, 16, C, 4), np.float32)
            np.put_along_axis(new, o, (away + p[:, :, :, None]).reshape(8, 16, C, 4), axis=2)
            made.append(new.reshape(128, 4 * C).astype(BF))
        now = made
    y = np.zeros((N, 128, C), np.float32)
    oc, osc = np.zeros((N, 128, 4 * C), np.uint8), np.zeros((N, 16, C), np.uint8)
    for r in range(N):
        q = mx_ref.quantize(now[r])
        y[r] = mx_ref.matmul(mx_ref.quantize(v[r]), q)
        oc[r], osc[r] = emit(q)
    return {"y": y, "oc": oc, "osc": osc}

@@ -1,0 +1,455 @@
+import numpy as np
+from concourse.mybir import dt, AluOpType, ActivationFunctionType
+
+C, K, E = 384, 64, 6
+STEP = [1, 2, 3]
+NV = 14
+TW = [384, 128, 176, 240, 304, 368]
+TO = [0, 384, 512, 688, 928, 1232]
+BIG = 2.0 ** 80
+X4, U8, U16, BF, F32, I32 = "float8_e4m3fn_x4", "uint8", "uint16", "bfloat16", "float32", "int32"
+
+_S = {
+    "x0": (1536, BF), "xt": (1536, BF), "qx": (384, X4), "sx": (384, U8),
+    "ut": (512, BF), "qu0": (128, X4), "su0": (128, U8), "qug": (128, X4), "sug": (128, U8),
+    "qu4": (512, X4), "su4": (512, U8),
+    "vt": (512, BF), "qv": (128, X4), "sv": (128, U8), "wq": (512, X4), "wsc": (512, U8),
+    "ones": (516, BF), "comb": (516, BF), "qe": (512, X4), "se": (512, U8),
+    "g0": (512, BF), "gt": (512, BF), "qg": (128, X4), "sg": (128, U8),
+    "bt": (6400, BF), "qb": (1600, X4), "sb": (1600, U8),
+    "xm": (384, BF), "bigs": (384, BF), "tbd": (384, BF), "tb2": (384, BF), "k1": (384, BF), "keep": (384, BF), "k2": (384, BF),
+    "ip": (8, I32), "pf": (16, F32), "uli": (40, I32), "ulj": (32, I32), "ulg": (8, U16), "ul4": (32, U16),
+    "c0": (24, F32), "c1": (24, F32), "vals": (384, BF), "ctab": (384, BF),
+    "m0": (96, F32), "m1": (96, F32), "m2": (96, I32), "mcu": (96, U16),
+    "o0": (2, F32), "ogu": (2, U16),
+    "md": (384, F32), "fill": (384, F32), "nu": (3 * 368, BF), "jr": (256 * 16, BF), "dj": (384, BF),
+    "racc": (24, F32), "pre": (24, F32), "pre2": (24, F32), "md2": (384, BF), "cs": (384, BF),
+    "posf": (24, F32), "posu": (24, U16), "sw": (416, BF), "tt": (768, BF), "ou": (32, U16),
+    "ts": (1536, BF), "am": (1792, BF), "am2": (1792, BF), "so": (1536, BF), "mt": (512, BF), "zt": (512, BF),
+    "dev": (3072, F32), "rk": (24, F32), "rku": (24, U16), "ce": (24, F32), "ci": (24, I32), "cu": (24, U16),
+    "rr": (384, BF), "rt": (384, BF), "blu": (24, U16),
+    "pz": (256, BF), "pc": (1536, BF), "va": (128, F32), "fl": (128, BF), "fr": (384, BF), "ft": (384, BF),
+    "offf": (24, F32), "offu": (24, U16), "ys": (384, F32),
+}
+for _t in range(3):
+    _S["qm%d" % _t] = (192, X4)
+    _S["sm%d" % _t] = (192, U8)
+    _S["qz%d" % _t] = (192, X4)
+    _S["sz%d" % _t] = (192, U8)
+SCRATCH = {k: ("sbuf", [128, n], d) for k, (n, d) in _S.items()}
+SCRATCH["ps"] = ("psum", [128, 4096], F32)
+SEMAPHORES = (["cv", "ca", "cp", "cg", "go", "lx", "lu", "lw", "lv", "so1", "so2", "so3", "so4"]
+              + ["%s%d" % (k, t) for k in ("rm", "rz", "lm", "lz", "dw", "dx") for t in range(3)])
+
+A = AluOpType
+AF = ActivationFunctionType
+
+
+def rank_program(g, core, T, topo):
+    rank = T.rank_of(core)
+    if rank is None:
+        return
+    n_ranks = len(T.cores)
+
+    eng = {"v": g.vector, "a": g.scalar, "p": g.tensor, "g": g, "s": g.sync}
+    csem = {"v": "cv", "a": "ca", "p": "cp", "g": "cg"}
+    total = {}
+    clock = {q: {} for q in eng}
+    ops = []
+    width = {k: n for k, (n, d) in _S.items()}
+    width["ps"] = 8
+    lastw = {k: np.full(n, -1) for k, n in width.items()}
+    lastr = {k: {} for k in width}
+
+    def S(name, a=0, b=None, st=1, p=None):
+        b = _S[name][0] if b is None else b
+        rows = slice(None) if p is None else slice(p[0], p[1])
+        ap = T[name][rows, a:b] if st == 1 else T[name][rows, a:b:st]
+        return {"ap": ap, "acc": [(name, np.arange(a, b, st))]}
+
+    def P(bank, a, b):
+        return {"ap": T["ps"][:, 512 * bank + a:512 * bank + b], "acc": [("ps", np.array([bank]))]}
+
+    def ind(win, off, words=False):
+        ap = win["ap"].bitcast(dt.uint32) if words else win["ap"]
+        return {"ap": ap.indirect(off["ap"]), "acc": win["acc"], "off": off["acc"]}
+
+    def order(q, key, reads, writes, chain=False):
+        deps = set()
+        for name, cols in reads:
+            deps.update(int(i) for i in lastw[name][cols])
+            if name == "ps":
+                for k2, arr in lastr[name].items():
+                    if k2 != key:
+                        deps.update(int(i) for i in arr[cols])
+        for name, cols in writes:
+            if not chain:
+                deps.update(int(i) for i in lastw[name][cols])
+            for arr in lastr[name].values():
+                deps.update(int(i) for i in arr[cols])
+        deps.discard(-1)
+        for i in sorted(deps, reverse=True):
+            sem, cnt, clk = ops[i]
+            if clock[q].get(sem, 0) < cnt:
+                eng[q].wait_ge(T.sem[sem], cnt)
+                for s2, c2 in clk.items():
+                    if clock[q].get(s2, 0) < c2:
+                        clock[q][s2] = c2
+
+    def note(q, key, sem, inc, reads, writes):
+        total[sem] = total.get(sem, 0) + inc
+        clk = dict(clock[q]) if q else {}
+        clk[sem] = total[sem]
+        ops.append((sem, total[sem], clk))
+        for name, cols in reads:
+            if key not in lastr[name]:
+                lastr[name][key] = np.full(width[name], -1)
+            lastr[name][key][cols] = len(ops) - 1
+        for name, cols in writes:
+            lastw[name][cols] = len(ops) - 1
+
+    def run(q, call, outs, ins, chain=False):
+        reads, writes = [], []
+        for d in ins:
+            if isinstance(d, dict):
+                reads += d["acc"] + d.get("off", [])
+        for d in outs:
+            writes += d["acc"]
+            reads += d.get("off", [])
+        order(q, q, reads, writes, chain)
+        call().then_inc(T.sem[csem[q]], 1)
+        note(q, q, csem[q], 1, reads, writes)
+
+    def ap(d):
+        return d["ap"] if isinstance(d, dict) else d
+
+    def dmas(q, sem, pairs, tracked=True):
+        reads, writes = [], []
+        for o, i in pairs:
+            writes += o["acc"]
+            reads += i["acc"]
+        order(q, sem, reads, writes if tracked else [])
+        for o, i in pairs:
+            eng[q].dma_start(o["ap"], i["ap"]).then_inc(T.sem[sem], 16)
+        note(q, sem, sem, 16 * len(pairs), reads, writes)
+
+    def hbm(a):
+        return {"ap": a, "acc": []}
+
+    def bytes_of(d):
+        return {"ap": d["ap"].bitcast(dt.uint8), "acc": d["acc"]}
+
+    def memset(o, c):
+        run("v", lambda: g.vector.memset(o["ap"], c), [o], [])
+
+    def copy(o, i):
+        run("v", lambda: g.vector.tensor_copy(o["ap"], i["ap"]), [o], [i])
+
+    def tten(o, a, b, op):
+        run("v", lambda: g.vector.tensor_tensor(o["ap"], a["ap"], b["ap"], op), [o], [a, b])
+
+    def tsc(o, a, s1, op0, s2=None, op1=None):
+        if op1 is None:
+            run("v", lambda: g.vector.tensor_scalar(o["ap"], a["ap"], ap(s1), None, op0), [o], [a, s1])
+        else:
+            run("v", lambda: g.vector.tensor_scalar(o["ap"], a["ap"], ap(s1), ap(s2), op0, op1), [o], [a, s1, s2])
+
+    def scan(o, d0, d1, op0, op1):
+        run("v", lambda: g.vector.tensor_tensor_scan(o["ap"], d0["ap"], d1["ap"], 0.0, op0, op1), [o], [d0, d1])
+
+    def turn(o, i):
+        run("v", lambda: g.vector.transpose(o["ap"], i["ap"]), [o], [i])
+
+    def quant(qn, sn, a, n, tile):
+        qo, so_ = S(qn, a, a + n), S(sn, a, a + n)
+        run("v", lambda: g.vector.quantize_mx(qo["ap"], so_["ap"], tile["ap"]), [qo, so_], [tile])
+
+    def act(o, i, func=AF.Copy, bias=None, scale=None, acc=None):
+        kw = {}
+        if bias is not None:
+            kw["bias"] = ap(bias)
+        if scale is not None:
+            kw["scale"] = scale
+        if acc is not None:
+            kw["accum_out"] = acc["ap"]
+        run("a", lambda: g.scalar.activation(o["ap"], i["ap"], func, **kw), [o] + ([acc] if acc else []), [i, bias])
+
+    def mm(bank, lq, ls, la, rq, rs, ra, n, start=True, stop=True):
+        o = P(bank, 0, n)
+        a, b, c, d = S(lq, la, la + 128), S(ls, la, la + 128), S(rq, ra, ra + n), S(rs, ra, ra + n)
+        run("p", lambda: g.tensor.matmul_mx(o["ap"], a["ap"], b["ap"], c["ap"], d["ap"], start, stop), [o], [a, b, c, d], chain=not start)
+
+    def iota(o, pat, base, cm, small=False):
+        if small:
+            run("g", lambda: g.iota(o["ap"], pat, base, cm, allow_small_or_imprecise_dtypes=True), [o], [])
+        else:
+            run("g", lambda: g.iota(o["ap"], pat, base, cm), [o], [])
+
+    def select(o, i, pat, op, fill, base, cm):
+        run("g", lambda: g.affine_select(o["ap"], i["ap"], pat, op, fill, base, cm), [o], [i])
+
+    def pick(qo, so_, off, on_scalar):
+        src = ind(S("qu0"), off, True)
+        run("v", lambda: g.vector.tensor_copy(qo["ap"].bitcast(dt.uint32), src["ap"]), [qo], [src])
+        if on_scalar:
+            act(so_, ind(S("su0"), off))
+        else:
+            copy(so_, ind(S("su0"), off))
+
+    def engines(src, dst):
+        e = topo.engines(src, dst)[:8]
+        return sum(1 << k for k in e), len(e)
+
+    def send(qn, sn, dst, rsem, lsem):
+        rid, pid, _ = topo.addr(dst)
+        mask, n = engines(core, dst)
+        qi, si = S(qn, 64, 128), S(sn, 64, 128)
+        order("g", lsem, qi["acc"] + si["acc"], [])
+        g.remote_dma(T[qn][:, 128:192].bitcast(dt.uint8), qi["ap"].bitcast(dt.uint8), T.sem[rsem], T.sem[lsem], pid, rid, mask)
+        g.remote_dma(T[sn][:, 128:192], si["ap"], T.sem[rsem], T.sem[lsem], pid, rid, mask)
+        note("g", lsem, lsem, 2 * n, qi["acc"] + si["acc"], [])
+
+    def arrives(qn, sn, src, rsem):
+        note(None, rsem, rsem, 2 * engines(src, core)[1], [], S(qn, 128, 192)["acc"] + S(sn, 128, 192)["acc"])
+
+    def slot(c, n):
+        return S("bt", 4 * TO[c // 4] + c % 4, 4 * (TO[c // 4] + n), 4)
+
+    def col(name, j):
+        return S(name, j, j + 1)
+
+    for t in range(3):
+        arrives("qm%d" % t, "sm%d" % t, T.cores[(rank - STEP[t]) % n_ranks], "rm%d" % t)
+        arrives("qz%d" % t, "sz%d" % t, T.cores[(rank + STEP[t]) % n_ranks], "rz%d" % t)
+
+    dmas("s", "lu", [(S("ut"), hbm(T.u[:]))])
+    dmas("s", "lx", [(S("x0"), hbm(T.x[:]))])
+    order("s", "lx", S("x0")["acc"], [])
+    dmas("s", "lw", [(bytes_of(S("wq")), hbm(T.wc[:])), (S("wsc"), hbm(T.ws[:]))])
+    dmas("s", "lv", [(S("vt"), hbm(T.v[:]))])
+
+    memset(S("ones"), 1.0)
+    act(S("bigs"), S("ones", 0, C), scale=BIG)
+    iota(S("ip", 0, 1), [[1, 1]], 0, 1)
+    iota(S("uli", 0, 8), [[16, 8]], 0, 0)
+    iota(S("xm"), [[0, 24], [1, 16]], 0, 0, True)
+    select(S("comb"), S("ones"), [[1, 516]], A.is_equal, 0.0, -3, -4)
+    iota(S("c0"), [[-16, 24]], 240, 0, True)
+    iota(S("o0"), [[256, 2]], 0, 0, True)
+    select(S("g0"), S("ones", 0, 512), [[-16, 8], [0, 64]], A.is_ge, 0.0, 0, 1)
+    select(S("gt"), S("g0"), [[16, 8], [0, 64]], A.is_ge, 0.0, 15, -1)
+    select(S("keep"), S("ones", 0, C), [[0, 24], [1, 16]], A.not_equal, 0.0, 0, 0)
+    iota(S("vals"), [[1, 384]], -128, 0, True)
+    select(S("k2"), S("bigs"), [[0, 64], [1, 6]], A.not_equal, -BIG, 0, 0)
+    iota(S("m0"), [[16, 96]], 0, 0, True)
+    iota(S("ctab"), [[1, 64], [0, 6]], 0, 0, True)
+    iota(S("uli", 8, 40), [[16, 4], [32, 4], [0, 2]], 112, 0)
+
+    def zero(o, n):
+        act(o, S("ones", 0, n), scale=0.0)
+    for t in range(1, 4):
+        zero(slot(t, 384), 384)
+    for k in range(1, 6):
+        zero(S("bt", 4 * (TO[k] + 64 * k), 4 * (TO[k] + TW[k])), 4 * (TW[k] - 64 * k))
+    zero(S("jr", 255, 256), 1)
+
+    memset(S("k1"), -BIG * 1024)
+    for j, m in enumerate([31, 16, 15, 1]):
+        tsc(col("ip", 1 + j), col("ip", 0), m, A.bitwise_and)
+    memset(S("k1", 0, 384, 16), BIG * 1024)
+    copy(S("pf", 0, 5), S("ip", 0, 5))
+    copy(S("ulg"), S("uli", 0, 8))
+    tsc(col("pf", 5), col("pf", 3), 16.0, A.mult, col("pf", 2), A.add)
+    tsc(col("pf", 6), col("pf", 2), 4.0, A.mult)
+    tsc(col("pf", 7), col("pf", 3), 2.5, A.subtract)
+    tsc(col("pf", 8), col("pf", 4), 368.0, A.mult, col("pf", 5), A.add)
+    tsc(S("tbd"), S("xm"), col("pf", 3), A.not_equal, 2 * BIG, A.mult)
+    tsc(S("tb2"), S("tbd"), 128.0, A.subtract)
+    quant("qu0", "su0", 0, 128, S("ut"))
+    pick(S("qug"), S("sug"), S("ulg"), False)
+    for b in range(4):
+        quant("qe", "se", 128 * b, 128, S("comb", 3 - b, 515 - b))
+
+    H = 16 * (NV + 1)
+    for t in range(3):
+        first = t == 0
+        qm, sm, qz, sz = "qm%d" % t, "sm%d" % t, "qz%d" % t, "sz%d" % t
+        xs = "x0" if first else "xt"
+        quant("qx", "sx", H, C - H, S(xs, 4 * H, 4 * C))
+        mm(7, "qug", "sug", 0, "qx", "sx", H, C - H)
+        quant("qx", "sx", 0, H, S(xs, 0, 4 * H))
+        mm(4, "qug", "sug", 0, "qx", "sx", 0, H)
+        mm(5, "qug", "sug", 0, "qx", "sx", 0, C)
+        for b in range(4):
+            mm(b, "qe", "se", 128 * b, "qx", "sx", 0, C)
+        if first:
+            tsc(S("c1"), S("c0"), col("pf", 1), A.add)
+            tsc(S("ogu"), S("o0"), col("pf", 8), A.add, 767.0, A.min)
+        tten(S("md", H, C), P(7, 0, C - H), S("tbd", H, C), A.add)
+        scan(S("fill", H, C), S("k1", H, C), S("md", H, C), A.max, A.min)
+        tten(S("md", 0, H), P(4, 0, H), S("tbd", 0, H), A.add)
+        scan(S("fill", 0, H), S("k1", 0, H), S("md", 0, H), A.max, A.min)
+        rows = list(range(23, NV, -1))
+        for i in range(len(rows) + 1):
+            if i < len(rows):
+                c = rows[i]
+                act(S("nu", 368 * (i % 3), 368 * (i % 3) + 16 * c), P(5, 0, 16 * c), AF.Sign, col("fill", 16 * c + 15), -1.0)
+            if i > 0:
+                c = rows[i - 1]
+                k = (i - 1) % 3
+                act(slot(c, 16 * c), S("nu", 368 * k, 368 * k + 16 * c), AF.Sign, 1.0, -1.0, col("racc", c))
+        if first:
+            zero(S("sw"), 416)
+        for b in range(4):
+            act(S("ts", C * b, C * b + C), P(b, 0, C))
+        if first:
+            zero(S("mt", 0, 256), 256)
+            zero(S("zt", 0, 256), 256)
+
+        done = []
+
+        def sums(k):
+            quant("qb", "sb", TO[k], TW[k], S("bt", 4 * TO[k], 4 * (TO[k] + TW[k])))
+            if first and not done:
+                quant("qg", "sg", 0, 128, S("gt"))
+            done.append(k)
+            mm(6, "qg", "sg", 0, "qb", "sb", TO[k], TW[k], len(done) == 1, len(done) == 6)
+
+        def rowsum(c):
+            scan(S("jr", 256 * (c + 1) - 16 * c, 256 * (c + 1)), slot(c, 16 * c), slot(c, 16 * c), A.add, A.max)
+
+        def vrows(cs, later=()):
+            for i in range(len(cs) + 1):
+                if i < len(cs):
+                    c = cs[i]
+                    tsc(slot(c, 16 * c), P(4, 0, 16 * c), col("fill", 16 * c + 15), A.is_ge)
+                if i > 0 and cs[i - 1] not in later:
+                    rowsum(cs[i - 1])
+
+        vrows(list(range(NV, 7, -1)))
+        tten(slot(0, H), P(4, 0, H), S("fill", 0, H), A.is_gt)
+        tten(S("bt", 4 * H, 4 * C, 4), P(7, 0, C - H), S("fill", H, C), A.is_gt)
+        vrows([3, 2, 1])
+        sums(0)
+        sums(5)
+        sums(2)
+        vrows([7, 6, 5, 4])
+        sums(1)
+        scan(S("dj"), S("keep"), slot(0, C), A.mult, A.add)
+        sums(4)
+        sums(3)
+        tten(S("pre2"), S("c1"), S("dj", 15, C, 16), A.add)
+        tten(S("pre", 0, NV + 1), S("pre2", 0, NV + 1), S("jr", 255, 256 * (NV + 1), 256), A.add)
+        tten(S("md2"), P(6, 0, C), S("tb2"), A.add)
+        tten(S("pre", NV + 1, 24), S("pre2", NV + 1, 24), S("racc", NV + 1, 24), A.add)
+        scan(S("cs"), S("k1"), S("md2"), A.max, A.min)
+        tten(S("posf"), S("pre"), S("cs", 15, C, 16), A.subtract)
+        copy(S("posu"), S("posf"))
+        copy(ind(S("sw", 0, 400), S("posu")), S("vals"))
+        turn(S("tt", 0, C), S("sw", 0, C))
+        turn(S("tt", C, 2 * C), S("sw", 16, 16 + C))
+        tsc(S("ou"), ind(S("tt"), S("ogu")), 128.0, A.add)
+
+        def win(b):
+            return S("ts", C * b, C * b + C)
+
+        def cells(b):
+            scan(S("so", C * b, C * b + C), S("k2"), S("am", C * b, C * b + C), A.min, A.max)
+
+        act(S("am", C, 2 * C), ind(win(1), S("ou", 0, 24)))
+        act(S("am", 2 * C, 3 * C), ind(win(2), S("ou", 0, 24)))
+        act(S("am", 3 * C + 192, 4 * C), ind(win(3), S("ou", 12, 24)))
+        copy(S("am", 0, C), ind(win(0), S("ou", 0, 24)))
+        copy(S("am", 3 * C, 3 * C + 192), ind(win(3), S("ou", 0, 12)))
+        for b in range(4):
+            cells(b)
+        for b in range(3):
+            act(S("mt", 256 + b, 512, 4), S("so", C * b + 5, C * b + C, 6))
+        copy(S("mt", 259, 512, 4), S("so", 3 * C + 5, 4 * C, 6))
+        quant(qm, sm, 0, 128, S("mt"))
+        send(qm, sm, T.cores[(rank + STEP[t]) % n_ranks], "rm%d" % t, "lm%d" % t)
+        g.sem_inc(T.sem["go"], 1)
+        total["go"] = t + 1
+        act(S("am", 1536, 1792), S("so", 5, 1536, 6), scale=-1.0)
+        pairs = []
+        for gr in range(8):
+            e = gr ^ 1 if t % 2 == 0 else (gr + 1 if gr % 2 else gr - 1) % 8
+            pairs.append((S("am2", p=(16 * gr, 16 * gr + 16)), S("am", p=(16 * e, 16 * e + 16))))
+        g.sync.wait_ge(T.sem["go"], t + 1)
+        dmas("s", "dw%d" % t, pairs)
+        tsc(S("rku"), S("posf"), col("pf", 2), A.subtract)
+        if first:
+            tsc(S("m1"), S("m0"), col("pf", 7), A.add, 1.0 / 6.0, A.mult)
+            copy(S("m2"), S("m1"))
+            copy(S("mcu"), S("m2"))
+        if t % 2:
+            act(S("rr"), ind(S("ctab"), S("rku")), AF.Identity, col("pf", 6))
+        else:
+            act(S("rr"), ind(S("ctab"), S("rku")))
+        for h in range(2):
+            tten(S("dev", 768 * h, 768 * h + 768), ind(S("am", 1536, 1792), S("mcu", 48 * h, 48 * h + 48)), S("am", 768 * h, 768 * h + 768), A.add)
+
+        for b in range(4):
+            mm(b, "wq", "wsc", 128 * b, qm, sm, 64, 128)
+        for b in range(4):
+            if b % 2:
+                tsc(S("zt", 256 + b, 512, 4), P(b, 64, 128), 0.015625, A.mult)
+            else:
+                act(S("zt", 256 + b, 512, 4), P(b, 64, 128), scale=0.015625)
+        quant(qz, sz, 0, 128, S("zt"))
+        send(qz, sz, T.cores[(rank - STEP[t]) % n_ranks], "rz%d" % t, "lz%d" % t)
+
+        tsc(S("rk"), S("posf"), col("pf", 2), A.subtract)
+        turn(S("rt"), S("rr"))
+        tsc(S("ce"), S("rk"), 2.5, A.subtract, 1.0 / 6.0, A.mult)
+        tsc(S("blu"), S("rt", 0, C, 16), 0.0, A.add)
+        copy(S("ci"), S("ce"))
+        if first:
+            tsc(S("ulj"), S("uli", 8, 40), 127, A.bitwise_and)
+        copy(S("cu"), S("ci"))
+        if first:
+            copy(S("ul4"), S("ulj"))
+            pick(S("qu4", 128, 384), S("su4", 128, 384), S("ul4", 8, 24), True)
+        if t == 1:
+            pick(S("qu4", 0, 128), S("su4", 0, 128), S("ul4", 0, 8), True)
+            pick(S("qu4", 384, 512), S("su4", 384, 512), S("ul4", 24, 32), True)
+        if t == 2:
+            quant("qv", "sv", 0, 128, S("vt"))
+        for h in range(2):
+            tten(S("dev", 1536 + 768 * h, 1536 + 768 * h + 768), ind(S("am2", 1536, 1792), S("mcu", 48 * h, 48 * h + 48)), S("am2", 768 * h, 768 * h + 768), A.add)
+
+        nf = 2 if t % 2 else 1
+        for h in range(nf):
+            lo = 2 * h if t % 2 else 1
+            mm(4 + 2 * h, "qu4", "su4", 128 * lo, qz, sz, 64, 128)
+            mm(5 + 2 * h, "qu4", "su4", 128 * lo + 128, qz, sz, 64, 128)
+        for b in range(4):
+            mm(b, "qe", "se", 128 * b, qz, sz, 64, 128)
+        copy(S("va", 0, 64), P(4, 64, 128))
+        if nf == 2:
+            act(S("va", 64, 128), P(6, 64, 128))
+        for b in range(4):
+            act(S("pz", 64 * b, 64 * b + 64), P(b, 64, 128))
+            act(S("pc", C * b, C * b + C), ind(S("pz", 64 * b, 64 * b + 64), S("cu")))
+        for h in range(nf):
+            tten(S("fl", 64 * h, 64 * h + 64), S("va", 64 * h, 64 * h + 64), P(5 + 2 * h, 64, 128), A.is_lt)
+        tsc(S("fr"), ind(S("fl", 0, 64 * nf), S("blu")), 1536.0, A.mult)
+        turn(S("ft"), S("fr"))
+        tten(S("offf"), S("ft", 0, C, 16), S("rk"), A.add)
+        copy(S("offu"), S("offf"))
+        for b in range(4):
+            tten(S("xt", b, 1536, 4), ind(S("dev", C * b, C * b + 1920), S("offu")), S("pc", C * b, C * b + C), A.add)
+
+    quant("qx", "sx", 0, 192, S("xt", 0, 768))
+    mm(4, "qv", "sv", 0, "qx", "sx", 0, 192)
+    quant("qx", "sx", 192, 192, S("xt", 768, 1536))
+    mm(5, "qv", "sv", 0, "qx", "sx", 192, 192)
+    act(S("ys", 0, 192), P(4, 0, 192))
+    copy(S("ys", 192, C), P(5, 0, 192))
+    sc = [(hbm(T.osc[4 * k:4 * k + 4, :]), S("sx", p=(32 * k, 32 * k + 4))) for k in range(4)]
+    dmas("a", "so4", [(hbm(T.y[:, 0:192]), S("ys", 0, 192))])
+    dmas("s", "so1", [(hbm(T.oc[:]), bytes_of(S("qx")))])
+    dmas("s", "so3", [(hbm(T.y[:, 192:C]), S("ys", 192, C))])
+    dmas("a", "so2", sc)
+    for sem, cnt in total.items():
+        g.wait_ge(T.sem[sem], cnt)

@@ -3,10 +3,16 @@ from concourse.mybir import dt, AluOpType, ActivationFunctionType
 
 C, K, E = 384, 64, 6
 STEP = [1, 2, 3]
-NV = 14
-TW = [384, 128, 176, 240, 304, 368]
-TO = [0, 384, 512, 688, 928, 1232]
+NV = 15
+NS, NT = 7, 15
+AFTER = {9: [0, 3], 5: [4], 3: [1], 1: [2, 5]}
+GV, FV = 14, 14
+H = 256
+TW = [384, 320, 256, 192, 128, 128]
+TO = [0, 384, 704, 960, 1216, 1344]
+LAST = 256
 BIG = 2.0 ** 80
+WHOLE = 1.5 * 2.0 ** 23
 X4, U8, U16, BF, F32, I32 = "float8_e4m3fn_x4", "uint8", "uint16", "bfloat16", "float32", "int32"
 
 _S = {
@@ -16,17 +22,17 @@ _S = {
     "vt": (512, BF), "qv": (128, X4), "sv": (128, U8), "wq": (512, X4), "wsc": (512, U8),
     "ones": (516, BF), "comb": (516, BF), "qe": (512, X4), "se": (512, U8),
     "g0": (512, BF), "gt": (512, BF), "qg": (128, X4), "sg": (128, U8),
-    "bt": (6400, BF), "qb": (1600, X4), "sb": (1600, U8),
-    "xm": (384, BF), "bigs": (384, BF), "tbd": (384, BF), "tb2": (384, BF), "k1": (384, BF), "keep": (384, BF), "k2": (384, BF),
+    "bt": (5888, BF), "qb": (1472, X4), "sb": (1472, U8),
+    "xm": (384, BF), "tbd": (384, BF), "i2": (384, BF), "tb2": (384, BF), "k1": (384, BF), "keep": (384, BF), "k2": (384, BF),
     "ip": (8, I32), "pf": (16, F32), "uli": (40, I32), "ulj": (32, I32), "ulg": (8, U16), "ul4": (32, U16),
-    "c0": (24, F32), "c1": (24, F32), "vals": (384, BF), "ctab": (384, BF),
-    "m0": (96, F32), "m1": (96, F32), "m2": (96, I32), "mcu": (96, U16),
+    "vals": (384, BF), "ctab": (384, BF),
+    "m0": (24, F32), "m1": (24, F32), "m2": (24, F32), "mcu": (24, U16),
     "o0": (2, F32), "ogu": (2, U16),
-    "md": (384, F32), "fill": (384, F32), "nu": (3 * 368, BF), "jr": (256 * 16, BF), "dj": (384, BF),
-    "racc": (24, F32), "pre": (24, F32), "pre2": (24, F32), "md2": (384, BF), "cs": (384, BF),
+    "md": (384, F32), "fill": (384, F32), "nu": (3 * 368, BF), "jr": (512 * 17, BF), "junk": (512, BF),
+    "racc": (24, F32), "pre": (24, F32), "md2": (384, BF), "cs": (384, BF),
     "posf": (24, F32), "posu": (24, U16), "sw": (416, BF), "tt": (768, BF), "ou": (32, U16),
-    "ts": (1536, BF), "am": (1792, BF), "am2": (1792, BF), "so": (1536, BF), "mt": (512, BF), "zt": (512, BF),
-    "dev": (3072, F32), "rk": (24, F32), "rku": (24, U16), "ce": (24, F32), "ci": (24, I32), "cu": (24, U16),
+    "ts": (1536, BF), "am": (1536, BF), "so": (1536, BF), "mt": (512, BF), "zt": (512, BF),
+    "dev": (3072, F32), "rk": (24, F32), "rku": (24, U16), "ce": (24, F32), "cu": (24, U16),
     "rr": (384, BF), "rt": (384, BF), "blu": (24, U16),
     "pz": (256, BF), "pc": (1536, BF), "va": (128, F32), "fl": (128, BF), "fr": (384, BF), "ft": (384, BF),
     "offf": (24, F32), "offu": (24, U16), "ys": (384, F32),
@@ -38,8 +44,8 @@ for _t in range(3):
     _S["sz%d" % _t] = (192, U8)
 SCRATCH = {k: ("sbuf", [128, n], d) for k, (n, d) in _S.items()}
 SCRATCH["ps"] = ("psum", [128, 4096], F32)
-SEMAPHORES = (["cv", "ca", "cp", "cg", "go", "lx", "lu", "lw", "lv", "so1", "so2", "so3", "so4"]
-              + ["%s%d" % (k, t) for k in ("rm", "rz", "lm", "lz", "dw", "dx") for t in range(3)])
+SEMAPHORES = (["cv", "ca", "cp", "cg", "lx", "lh", "lu", "lw", "lv", "so1", "so2", "so3", "so4", "so5", "so6"]
+              + ["%s%d" % (k, t) for k in ("rm", "rz", "lm", "lz", "dw", "dx", "dy") for t in range(3)])
 
 A = AluOpType
 AF = ActivationFunctionType
@@ -123,12 +129,12 @@ def rank_program(g, core, T, topo):
     def ap(d):
         return d["ap"] if isinstance(d, dict) else d
 
-    def dmas(q, sem, pairs, tracked=True):
+    def dmas(q, sem, pairs):
         reads, writes = [], []
         for o, i in pairs:
             writes += o["acc"]
             reads += i["acc"]
-        order(q, sem, reads, writes if tracked else [])
+        order(q, sem, reads, writes)
         for o, i in pairs:
             eng[q].dma_start(o["ap"], i["ap"]).then_inc(T.sem[sem], 16)
         note(q, sem, sem, 16 * len(pairs), reads, writes)
@@ -154,8 +160,8 @@ def rank_program(g, core, T, topo):
         else:
             run("v", lambda: g.vector.tensor_scalar(o["ap"], a["ap"], ap(s1), ap(s2), op0, op1), [o], [a, s1, s2])
 
-    def scan(o, d0, d1, op0, op1):
-        run("v", lambda: g.vector.tensor_tensor_scan(o["ap"], d0["ap"], d1["ap"], 0.0, op0, op1), [o], [d0, d1])
+    def scan(o, d0, d1, op0, op1, init=0.0):
+        run("v", lambda: g.vector.tensor_tensor_scan(o["ap"], d0["ap"], d1["ap"], ap(init), op0, op1), [o], [d0, d1, init])
 
     def turn(o, i):
         run("v", lambda: g.vector.transpose(o["ap"], i["ap"]), [o], [i])
@@ -188,16 +194,13 @@ def rank_program(g, core, T, topo):
     def select(o, i, pat, op, fill, base, cm):
         run("g", lambda: g.affine_select(o["ap"], i["ap"], pat, op, fill, base, cm), [o], [i])
 
-    def pick(qo, so_, off, on_scalar):
+    def pick(qo, so_, off):
         src = ind(S("qu0"), off, True)
         run("v", lambda: g.vector.tensor_copy(qo["ap"].bitcast(dt.uint32), src["ap"]), [qo], [src])
-        if on_scalar:
-            act(so_, ind(S("su0"), off))
-        else:
-            copy(so_, ind(S("su0"), off))
+        act(so_, ind(S("su0"), off))
 
     def engines(src, dst):
-        e = topo.engines(src, dst)[:8]
+        e = topo.engines(src, dst)
         return sum(1 << k for k in e), len(e)
 
     def send(qn, sn, dst, rsem, lsem):
@@ -213,64 +216,70 @@ def rank_program(g, core, T, topo):
         note(None, rsem, rsem, 2 * engines(src, core)[1], [], S(qn, 128, 192)["acc"] + S(sn, 128, 192)["acc"])
 
     def slot(c, n):
-        return S("bt", 4 * TO[c // 4] + c % 4, 4 * (TO[c // 4] + n), 4)
+        k, e = divmod(24 - c, 4)
+        return S("bt", 4 * TO[k] + e, 4 * (TO[k] + n), 4)
 
     def col(name, j):
         return S(name, j, j + 1)
+
+    def zero(o, n):
+        act(o, S("ones", 0, n), scale=0.0)
 
     for t in range(3):
         arrives("qm%d" % t, "sm%d" % t, T.cores[(rank - STEP[t]) % n_ranks], "rm%d" % t)
         arrives("qz%d" % t, "sz%d" % t, T.cores[(rank + STEP[t]) % n_ranks], "rz%d" % t)
 
     dmas("s", "lu", [(S("ut"), hbm(T.u[:]))])
-    dmas("s", "lx", [(S("x0"), hbm(T.x[:]))])
+    dmas("a", "lh", [(S("x0", 4 * H, 4 * C), hbm(T.x[:, 4 * H:4 * C]))])
+    dmas("s", "lx", [(S("x0", 0, 4 * H), hbm(T.x[:, 0:4 * H]))])
     order("s", "lx", S("x0")["acc"], [])
     dmas("s", "lw", [(bytes_of(S("wq")), hbm(T.wc[:])), (S("wsc"), hbm(T.ws[:]))])
     dmas("s", "lv", [(S("vt"), hbm(T.v[:]))])
 
     memset(S("ones"), 1.0)
-    act(S("bigs"), S("ones", 0, C), scale=BIG)
     iota(S("ip", 0, 1), [[1, 1]], 0, 1)
     iota(S("uli", 0, 8), [[16, 8]], 0, 0)
     iota(S("xm"), [[0, 24], [1, 16]], 0, 0, True)
     select(S("comb"), S("ones"), [[1, 516]], A.is_equal, 0.0, -3, -4)
-    iota(S("c0"), [[-16, 24]], 240, 0, True)
-    iota(S("o0"), [[256, 2]], 0, 0, True)
     select(S("g0"), S("ones", 0, 512), [[-16, 8], [0, 64]], A.is_ge, 0.0, 0, 1)
     select(S("gt"), S("g0"), [[16, 8], [0, 64]], A.is_ge, 0.0, 15, -1)
-    select(S("keep"), S("ones", 0, C), [[0, 24], [1, 16]], A.not_equal, 0.0, 0, 0)
+    iota(S("i2"), [[-16, 24], [1, 16]], 240, 0, True)
+    iota(S("o0"), [[256, 2]], 0, 0, True)
     iota(S("vals"), [[1, 384]], -128, 0, True)
-    select(S("k2"), S("bigs"), [[0, 64], [1, 6]], A.not_equal, -BIG, 0, 0)
-    iota(S("m0"), [[16, 96]], 0, 0, True)
+    iota(S("m0"), [[16, 24]], 0, 0, True)
     iota(S("ctab"), [[1, 64], [0, 6]], 0, 0, True)
     iota(S("uli", 8, 40), [[16, 4], [32, 4], [0, 2]], 112, 0)
 
-    def zero(o, n):
-        act(o, S("ones", 0, n), scale=0.0)
-    for t in range(1, 4):
-        zero(slot(t, 384), 384)
-    for k in range(1, 6):
-        zero(S("bt", 4 * (TO[k] + 64 * k), 4 * (TO[k] + TW[k])), 4 * (TW[k] - 64 * k))
-    zero(S("jr", 255, 256), 1)
+    def padding(k):
+        a, b = TO[k] + 16 * (21 - 4 * k), TO[k + 1] if k < 5 else TO[k] + TW[k]
+        zero(S("bt", 4 * a, 4 * b), 4 * (b - a))
 
+    for k in range(4):
+        padding(k)
     memset(S("k1"), -BIG * 1024)
     for j, m in enumerate([31, 16, 15, 1]):
         tsc(col("ip", 1 + j), col("ip", 0), m, A.bitwise_and)
-    memset(S("k1", 0, 384, 16), BIG * 1024)
+    memset(S("k1", 0, C, 16), BIG * 1024)
+    memset(S("keep"), 1.0)
     copy(S("pf", 0, 5), S("ip", 0, 5))
     copy(S("ulg"), S("uli", 0, 8))
+    memset(S("keep", 0, C, 16), 0.0)
     tsc(col("pf", 5), col("pf", 3), 16.0, A.mult, col("pf", 2), A.add)
     tsc(col("pf", 6), col("pf", 2), 4.0, A.mult)
     tsc(col("pf", 7), col("pf", 3), 2.5, A.subtract)
     tsc(col("pf", 8), col("pf", 4), 368.0, A.mult, col("pf", 5), A.add)
+    tsc(col("pf", 9), col("pf", 2), 128.0, A.add)
+    memset(S("k2"), -BIG)
     tsc(S("tbd"), S("xm"), col("pf", 3), A.not_equal, 2 * BIG, A.mult)
-    tsc(S("tb2"), S("tbd"), 128.0, A.subtract)
+    memset(S("k2", 0, C, E), BIG)
     quant("qu0", "su0", 0, 128, S("ut"))
-    pick(S("qug"), S("sug"), S("ulg"), False)
-    for b in range(4):
-        quant("qe", "se", 128 * b, 128, S("comb", 3 - b, 515 - b))
+    pick(S("qug"), S("sug"), S("ulg"))
+    for k in range(4, 6):
+        padding(k)
+    zero(col("racc", 0), 1)
+    zero(S("mt", 0, 256), 256)
+    zero(S("zt", 0, 256), 256)
 
-    H = 16 * (NV + 1)
     for t in range(3):
         first = t == 0
         qm, sm, qz, sz = "qm%d" % t, "sm%d" % t, "qz%d" % t, "sz%d" % t
@@ -280,14 +289,13 @@ def rank_program(g, core, T, topo):
         quant("qx", "sx", 0, H, S(xs, 0, 4 * H))
         mm(4, "qug", "sug", 0, "qx", "sx", 0, H)
         mm(5, "qug", "sug", 0, "qx", "sx", 0, C)
-        for b in range(4):
-            mm(b, "qe", "se", 128 * b, "qx", "sx", 0, C)
-        if first:
-            tsc(S("c1"), S("c0"), col("pf", 1), A.add)
-            tsc(S("ogu"), S("o0"), col("pf", 8), A.add, 767.0, A.min)
         tten(S("md", H, C), P(7, 0, C - H), S("tbd", H, C), A.add)
+        if first:
+            quant("qe", "se", 0, 128, S("comb", 3, 515))
         scan(S("fill", H, C), S("k1", H, C), S("md", H, C), A.max, A.min)
         tten(S("md", 0, H), P(4, 0, H), S("tbd", 0, H), A.add)
+        tten(S("bt", 4 * H, 4 * C, 4), P(7, 0, C - H), S("fill", H, C), A.is_gt)
+
         scan(S("fill", 0, H), S("k1", 0, H), S("md", 0, H), A.max, A.min)
         rows = list(range(23, NV, -1))
         for i in range(len(rows) + 1):
@@ -298,53 +306,59 @@ def rank_program(g, core, T, topo):
                 c = rows[i - 1]
                 k = (i - 1) % 3
                 act(slot(c, 16 * c), S("nu", 368 * k, 368 * k + 16 * c), AF.Sign, 1.0, -1.0, col("racc", c))
+
+        def row(c):
+            tsc(slot(c, 16 * c), P(4, 0, 16 * c), col("fill", 16 * c + 15), A.is_ge)
+
+        def inner(c):
+            return 512 - 16 + 16 * c + 15
+
+        def rowsum(c):
+            scan(S("jr", 512 * (c + 1) - 16 * c, 512 * (c + 1)), slot(c, 16 * c), slot(c, 16 * c), A.add, A.max)
+
+        low, high = [], []
+
+        def sums(k):
+            n = TW[k] + (64 if first and k == 3 else 0)
+            quant("qb", "sb", TO[k], n, S("bt", 4 * TO[k], 4 * (TO[k] + n)))
+            if k < 4:
+                high.append(k)
+                mm(6, "qg", "sg", 0, "qb", "sb", TO[k] + 128, max(128, TW[k] - 128), len(high) == 1, len(high) == 4)
+            low.append(k)
+            mm(7, "qg", "sg", 0, "qb", "sb", TO[k], 128, len(low) == 1, len(low) == 6)
+
+        if first:
+            for b in range(1, 4):
+                quant("qe", "se", 128 * b, 128, S("comb", 3 - b, 515 - b))
+        for b in range(4):
+            mm(b, "qe", "se", 128 * b, "qx", "sx", 0, C)
+        tten(slot(24, H), P(4, 0, H), S("fill", 0, H), A.is_gt)
+        row(NV)
+        scan(S("jr", inner(0) - 15, inner(0) - 15 + C), S("keep"), slot(24, C), A.mult, A.add)
+        for c in range(NV - 1, 0, -1):
+            row(c)
+            if NS <= c + 1 <= NT:
+                rowsum(c + 1)
+            if first and c == 9:
+                quant("qg", "sg", 0, 128, S("gt"))
+                scan(S("tb2"), S("i2"), S("tbd"), A.min, A.add, BIG)
+                tsc(S("ogu"), S("o0"), col("pf", 8), A.add, 767.0, A.min)
+            for k in AFTER.get(c, []):
+                sums(k)
+        for c in list(range(NV, NT, -1)) + list(range(NS - 1, 0, -1)):
+            act(S("junk", 256 * (c % 2), 256 * (c % 2) + 16 * c), slot(c, 16 * c), acc=col("racc", c))
         if first:
             zero(S("sw"), 416)
         for b in range(4):
-            act(S("ts", C * b, C * b + C), P(b, 0, C))
-        if first:
-            zero(S("mt", 0, 256), 256)
-            zero(S("zt", 0, 256), 256)
-
-        done = []
-
-        def sums(k):
-            quant("qb", "sb", TO[k], TW[k], S("bt", 4 * TO[k], 4 * (TO[k] + TW[k])))
-            if first and not done:
-                quant("qg", "sg", 0, 128, S("gt"))
-            done.append(k)
-            mm(6, "qg", "sg", 0, "qb", "sb", TO[k], TW[k], len(done) == 1, len(done) == 6)
-
-        def rowsum(c):
-            scan(S("jr", 256 * (c + 1) - 16 * c, 256 * (c + 1)), slot(c, 16 * c), slot(c, 16 * c), A.add, A.max)
-
-        def vrows(cs, later=()):
-            for i in range(len(cs) + 1):
-                if i < len(cs):
-                    c = cs[i]
-                    tsc(slot(c, 16 * c), P(4, 0, 16 * c), col("fill", 16 * c + 15), A.is_ge)
-                if i > 0 and cs[i - 1] not in later:
-                    rowsum(cs[i - 1])
-
-        vrows(list(range(NV, 7, -1)))
-        tten(slot(0, H), P(4, 0, H), S("fill", 0, H), A.is_gt)
-        tten(S("bt", 4 * H, 4 * C, 4), P(7, 0, C - H), S("fill", H, C), A.is_gt)
-        vrows([3, 2, 1])
-        sums(0)
-        sums(5)
-        sums(2)
-        vrows([7, 6, 5, 4])
-        sums(1)
-        scan(S("dj"), S("keep"), slot(0, C), A.mult, A.add)
-        sums(4)
-        sums(3)
-        tten(S("pre2"), S("c1"), S("dj", 15, C, 16), A.add)
-        tten(S("pre", 0, NV + 1), S("pre2", 0, NV + 1), S("jr", 255, 256 * (NV + 1), 256), A.add)
-        tten(S("md2"), P(6, 0, C), S("tb2"), A.add)
-        tten(S("pre", NV + 1, 24), S("pre2", NV + 1, 24), S("racc", NV + 1, 24), A.add)
-        scan(S("cs"), S("k1"), S("md2"), A.max, A.min)
-        tten(S("posf"), S("pre"), S("cs", 15, C, 16), A.subtract)
-        copy(S("posu"), S("posf"))
+            act(S("ts", C * b, C * b + C), P(b, 0, C), scale=-1.0)
+        copy(S("racc", NS, NT + 1), S("jr", 512 * (NS + 1) - 1, 512 * (NT + 1), 512))
+        tten(S("md2", 128, C), S("tb2", 128, C), P(6, 0, C - 128), A.subtract)
+        tten(S("md2", 0, 128), S("tb2", 0, 128), P(7, 0, 128), A.subtract)
+        scan(S("cs", 128, C), S("k1", 128, C), S("md2", 128, C), A.max, A.min)
+        scan(S("cs", 0, 128), S("k1", 0, 128), S("md2", 0, 128), A.max, A.min)
+        tten(S("pre"), S("jr", inner(0), inner(24), 16), S("racc"), A.add)
+        tten(S("posf"), S("pre"), S("cs", 15, C, 16), A.add)
+        tsc(S("posu"), S("posf"), col("pf", 9), A.add)
         copy(ind(S("sw", 0, 400), S("posu")), S("vals"))
         turn(S("tt", 0, C), S("sw", 0, C))
         turn(S("tt", C, 2 * C), S("sw", 16, 16 + C))
@@ -354,69 +368,74 @@ def rank_program(g, core, T, topo):
             return S("ts", C * b, C * b + C)
 
         def cells(b):
-            scan(S("so", C * b, C * b + C), S("k2"), S("am", C * b, C * b + C), A.min, A.max)
+            scan(S("so", C * b, C * b + C), S("k2"), S("am", C * b, C * b + C), A.max, A.min)
 
         act(S("am", C, 2 * C), ind(win(1), S("ou", 0, 24)))
         act(S("am", 2 * C, 3 * C), ind(win(2), S("ou", 0, 24)))
-        act(S("am", 3 * C + 192, 4 * C), ind(win(3), S("ou", 12, 24)))
+        act(S("am", 3 * C + 16 * GV, 4 * C), ind(win(3), S("ou", GV, 24)))
         copy(S("am", 0, C), ind(win(0), S("ou", 0, 24)))
-        copy(S("am", 3 * C, 3 * C + 192), ind(win(3), S("ou", 0, 12)))
+        copy(S("am", 3 * C, 3 * C + 16 * GV), ind(win(3), S("ou", 0, GV)))
         for b in range(4):
             cells(b)
         for b in range(3):
-            act(S("mt", 256 + b, 512, 4), S("so", C * b + 5, C * b + C, 6))
-        copy(S("mt", 259, 512, 4), S("so", 3 * C + 5, 4 * C, 6))
+            act(S("mt", 256 + b, 512, 4), S("so", C * b + 5, C * b + C, E), scale=-1.0)
+        tsc(S("mt", 259, 512, 4), S("so", 3 * C + 5, 4 * C, E), -1.0, A.mult)
+        if first:
+            tsc(S("m1"), S("m0"), col("pf", 7), A.add, 1.0 / E, A.mult)
         quant(qm, sm, 0, 128, S("mt"))
         send(qm, sm, T.cores[(rank + STEP[t]) % n_ranks], "rm%d" % t, "lm%d" % t)
-        g.sem_inc(T.sem["go"], 1)
-        total["go"] = t + 1
-        act(S("am", 1536, 1792), S("so", 5, 1536, 6), scale=-1.0)
-        pairs = []
-        for gr in range(8):
-            e = gr ^ 1 if t % 2 == 0 else (gr + 1 if gr % 2 else gr - 1) % 8
-            pairs.append((S("am2", p=(16 * gr, 16 * gr + 16)), S("am", p=(16 * e, 16 * e + 16))))
-        g.sync.wait_ge(T.sem["go"], t + 1)
-        dmas("s", "dw%d" % t, pairs)
-        tsc(S("rku"), S("posf"), col("pf", 2), A.subtract)
+
+        def dev(b):
+            tten(S("dev", C * b, C * b + C), ind(S("so", C * b, C * b + C), S("mcu")), S("am", C * b, C * b + C), A.subtract)
+
+        def swap(a, b, sem):
+            pairs = []
+            for gr in range(8):
+                e = gr ^ 1 if t % 2 == 0 else (gr + 1 if gr % 2 else gr - 1) % 8
+                pairs.append((S("dev", C * (4 + a), C * (4 + b), p=(16 * gr, 16 * gr + 16)), S("dev", C * a, C * b, p=(16 * e, 16 * e + 16))))
+            dmas("s", sem + str(t), pairs)
+
         if first:
-            tsc(S("m1"), S("m0"), col("pf", 7), A.add, 1.0 / 6.0, A.mult)
-            copy(S("m2"), S("m1"))
-            copy(S("mcu"), S("m2"))
+            tsc(S("m2"), S("m1"), WHOLE, A.add, WHOLE, A.subtract)
+        tsc(S("rku"), S("posf"), 128.0, A.add)
+        if first:
+            tsc(S("mcu"), S("m2"), float(E), A.mult, E - 1.0, A.add)
         if t % 2:
             act(S("rr"), ind(S("ctab"), S("rku")), AF.Identity, col("pf", 6))
         else:
             act(S("rr"), ind(S("ctab"), S("rku")))
-        for h in range(2):
-            tten(S("dev", 768 * h, 768 * h + 768), ind(S("am", 1536, 1792), S("mcu", 48 * h, 48 * h + 48)), S("am", 768 * h, 768 * h + 768), A.add)
+        dev(0)
+        if not first:
+            swap(0, 1, "dw")
+        else:
+            tsc(S("ulj"), S("uli", 8, 40), 127, A.bitwise_and)
+        dev(1)
+        if first:
+            copy(S("ul4"), S("ulj"))
+        dev(2)
+        if first:
+            pick(S("qu4"), S("su4"), S("ul4"))
 
         for b in range(4):
             mm(b, "wq", "wsc", 128 * b, qm, sm, 64, 128)
         for b in range(4):
-            if b % 2:
-                tsc(S("zt", 256 + b, 512, 4), P(b, 64, 128), 0.015625, A.mult)
-            else:
-                act(S("zt", 256 + b, 512, 4), P(b, 64, 128), scale=0.015625)
+            act(S("zt", 256 + b, 512, 4), P(b, 64, 128), scale=0.015625)
         quant(qz, sz, 0, 128, S("zt"))
         send(qz, sz, T.cores[(rank - STEP[t]) % n_ranks], "rz%d" % t, "lz%d" % t)
 
-        tsc(S("rk"), S("posf"), col("pf", 2), A.subtract)
+        dev(3)
+        order("s", "dx", S("dev", 3 * C, 4 * C)["acc"], [])
+        if first:
+            swap(0, 1, "dw")
+        swap(1, 3, "dx")
+        swap(3, 4, "dy")
         turn(S("rt"), S("rr"))
-        tsc(S("ce"), S("rk"), 2.5, A.subtract, 1.0 / 6.0, A.mult)
+        tsc(S("ce"), S("posf"), 125.5, A.add, 1.0 / E, A.mult)
+        tsc(S("rk"), S("posf"), 128.0, A.add)
         tsc(S("blu"), S("rt", 0, C, 16), 0.0, A.add)
-        copy(S("ci"), S("ce"))
+        tsc(S("cu"), S("ce"), WHOLE, A.add, WHOLE, A.subtract)
         if first:
-            tsc(S("ulj"), S("uli", 8, 40), 127, A.bitwise_and)
-        copy(S("cu"), S("ci"))
-        if first:
-            copy(S("ul4"), S("ulj"))
-            pick(S("qu4", 128, 384), S("su4", 128, 384), S("ul4", 8, 24), True)
-        if t == 1:
-            pick(S("qu4", 0, 128), S("su4", 0, 128), S("ul4", 0, 8), True)
-            pick(S("qu4", 384, 512), S("su4", 384, 512), S("ul4", 24, 32), True)
-        if t == 2:
             quant("qv", "sv", 0, 128, S("vt"))
-        for h in range(2):
-            tten(S("dev", 1536 + 768 * h, 1536 + 768 * h + 768), ind(S("am2", 1536, 1792), S("mcu", 48 * h, 48 * h + 48)), S("am2", 768 * h, 768 * h + 768), A.add)
 
         nf = 2 if t % 2 else 1
         for h in range(nf):
@@ -428,28 +447,33 @@ def rank_program(g, core, T, topo):
         copy(S("va", 0, 64), P(4, 64, 128))
         if nf == 2:
             act(S("va", 64, 128), P(6, 64, 128))
-        for b in range(4):
-            act(S("pz", 64 * b, 64 * b + 64), P(b, 64, 128))
-            act(S("pc", C * b, C * b + C), ind(S("pz", 64 * b, 64 * b + 64), S("cu")))
         for h in range(nf):
             tten(S("fl", 64 * h, 64 * h + 64), S("va", 64 * h, 64 * h + 64), P(5 + 2 * h, 64, 128), A.is_lt)
-        tsc(S("fr"), ind(S("fl", 0, 64 * nf), S("blu")), 1536.0, A.mult)
+        act(S("fr", 16 * FV, C), ind(S("fl", 0, 64 * nf), S("blu", FV, 24)), scale=1536.0)
+        copy(S("pz", 0, 64), P(0, 64, 128))
+        tsc(S("fr", 0, 16 * FV), ind(S("fl", 0, 64 * nf), S("blu", 0, FV)), 1536.0, A.mult)
         turn(S("ft"), S("fr"))
+        copy(S("pz", 64, 128), P(1, 64, 128))
         tten(S("offf"), S("ft", 0, C, 16), S("rk"), A.add)
+        copy(S("pz", 128, 192), P(2, 64, 128))
         copy(S("offu"), S("offf"))
-        for b in range(4):
-            tten(S("xt", b, 1536, 4), ind(S("dev", C * b, C * b + 1920), S("offu")), S("pc", C * b, C * b + C), A.add)
+        copy(S("pz", 192, 256), P(3, 64, 128))
+        for lo, hi in ([(0, C)] if t < 2 else [(0, LAST), (LAST, C)]):
+            for b in range(4):
+                act(S("pc", C * b + lo, C * b + hi), ind(S("pz", 64 * b, 64 * b + 64), S("cu", lo // 16, hi // 16)))
+                tten(S("xt", 4 * lo + b, 4 * hi, 4), ind(S("dev", C * b, C * b + 1920), S("offu", lo // 16, hi // 16)), S("pc", C * b + lo, C * b + hi), A.add)
+            if t == 2:
+                k = 0 if lo == 0 else 1
+                quant("qx", "sx", lo, hi - lo, S("xt", 4 * lo, 4 * hi))
+                mm(4 + k, "qv", "sv", 0, "qx", "sx", lo, hi - lo)
+                dmas("s", "so%d" % (1 + k), [(hbm(T.oc[:, 4 * lo:4 * hi]), bytes_of(S("qx", lo, hi)))])
 
-    quant("qx", "sx", 0, 192, S("xt", 0, 768))
-    mm(4, "qv", "sv", 0, "qx", "sx", 0, 192)
-    quant("qx", "sx", 192, 192, S("xt", 768, 1536))
-    mm(5, "qv", "sv", 0, "qx", "sx", 192, 192)
-    act(S("ys", 0, 192), P(4, 0, 192))
-    copy(S("ys", 192, C), P(5, 0, 192))
+    act(S("ys", 0, LAST), P(4, 0, LAST))
+    dmas("a", "so3", [(hbm(T.y[:, 0:LAST]), S("ys", 0, LAST))])
+    copy(S("ys", LAST, C), P(5, 0, C - LAST))
     sc = [(hbm(T.osc[4 * k:4 * k + 4, :]), S("sx", p=(32 * k, 32 * k + 4))) for k in range(4)]
-    dmas("a", "so4", [(hbm(T.y[:, 0:192]), S("ys", 0, 192))])
-    dmas("s", "so1", [(hbm(T.oc[:]), bytes_of(S("qx")))])
-    dmas("s", "so3", [(hbm(T.y[:, 192:C]), S("ys", 192, C))])
-    dmas("a", "so2", sc)
+    dmas("a", "so4", sc[0:2])
+    dmas("s", "so5", sc[2:4])
+    dmas("a", "so6", [(hbm(T.y[:, LAST:C]), S("ys", LAST, C))])
     for sem, cnt in total.items():
         g.wait_ge(T.sem[sem], cnt)

import numpy as np
from concourse.mybir import dt, AluOpType, ActivationFunctionType

C, K, E = 384, 64, 6
STEP = [1, 2, 3]
NV = 15
NS, NT = 7, 15
AFTER = {9: [0, 3], 5: [4], 3: [1], 1: [2, 5]}
GV, FV = 14, 14
H = 256
TW = [384, 320, 256, 192, 128, 128]
TO = [0, 384, 704, 960, 1216, 1344]
LAST = 256
BIG = 2.0 ** 80
WHOLE = 1.5 * 2.0 ** 23
X4, U8, U16, BF, F32, I32 = "float8_e4m3fn_x4", "uint8", "uint16", "bfloat16", "float32", "int32"

_S = {
    "x0": (1536, BF), "xt": (1536, BF), "qx": (384, X4), "sx": (384, U8),
    "ut": (512, BF), "qu0": (128, X4), "su0": (128, U8), "qug": (128, X4), "sug": (128, U8),
    "qu4": (512, X4), "su4": (512, U8),
    "vt": (512, BF), "qv": (128, X4), "sv": (128, U8), "wq": (512, X4), "wsc": (512, U8),
    "ones": (516, BF), "comb": (516, BF), "qe": (512, X4), "se": (512, U8),
    "g0": (512, BF), "gt": (512, BF), "qg": (128, X4), "sg": (128, U8),
    "bt": (5888, BF), "qb": (1472, X4), "sb": (1472, U8),
    "xm": (384, BF), "tbd": (384, BF), "i2": (384, BF), "tb2": (384, BF), "k1": (384, BF), "keep": (384, BF), "k2": (384, BF),
    "ip": (8, I32), "pf": (16, F32), "uli": (40, I32), "ulj": (32, I32), "ulg": (8, U16), "ul4": (32, U16),
    "vals": (384, BF), "ctab": (384, BF),
    "m0": (24, F32), "m1": (24, F32), "m2": (24, F32), "mcu": (24, U16),
    "o0": (2, F32), "ogu": (2, U16),
    "md": (384, F32), "fill": (384, F32), "nu": (3 * 368, BF), "jr": (512 * 17, BF), "junk": (512, BF),
    "racc": (24, F32), "pre": (24, F32), "md2": (384, BF), "cs": (384, BF),
    "posf": (24, F32), "posu": (24, U16), "sw": (416, BF), "tt": (768, BF), "ou": (32, U16),
    "ts": (1536, BF), "am": (1536, BF), "so": (1536, BF), "mt": (512, BF), "zt": (512, BF),
    "dev": (3072, F32), "rk": (24, F32), "rku": (24, U16), "ce": (24, F32), "cu": (24, U16),
    "rr": (384, BF), "rt": (384, BF), "blu": (24, U16),
    "pz": (256, BF), "pc": (1536, BF), "va": (128, F32), "fl": (128, BF), "fr": (384, BF), "ft": (384, BF),
    "offf": (24, F32), "offu": (24, U16), "ys": (384, F32),
}
for _t in range(3):
    _S["qm%d" % _t] = (192, X4)
    _S["sm%d" % _t] = (192, U8)
    _S["qz%d" % _t] = (192, X4)
    _S["sz%d" % _t] = (192, U8)
SCRATCH = {k: ("sbuf", [128, n], d) for k, (n, d) in _S.items()}
SCRATCH["ps"] = ("psum", [128, 4096], F32)
SEMAPHORES = (["cv", "ca", "cp", "cg", "lx", "lh", "lu", "lw", "lv", "so1", "so2", "so3", "so4", "so5", "so6"]
              + ["%s%d" % (k, t) for k in ("rm", "rz", "lm", "lz", "dw", "dx", "dy") for t in range(3)])

A = AluOpType
AF = ActivationFunctionType


def rank_program(g, core, T, topo):
    rank = T.rank_of(core)
    if rank is None:
        return
    n_ranks = len(T.cores)

    eng = {"v": g.vector, "a": g.scalar, "p": g.tensor, "g": g, "s": g.sync}
    csem = {"v": "cv", "a": "ca", "p": "cp", "g": "cg"}
    total = {}
    clock = {q: {} for q in eng}
    ops = []
    width = {k: n for k, (n, d) in _S.items()}
    width["ps"] = 8
    lastw = {k: np.full(n, -1) for k, n in width.items()}
    lastr = {k: {} for k in width}

    def S(name, a=0, b=None, st=1, p=None):
        b = _S[name][0] if b is None else b
        rows = slice(None) if p is None else slice(p[0], p[1])
        ap = T[name][rows, a:b] if st == 1 else T[name][rows, a:b:st]
        return {"ap": ap, "acc": [(name, np.arange(a, b, st))]}

    def P(bank, a, b):
        return {"ap": T["ps"][:, 512 * bank + a:512 * bank + b], "acc": [("ps", np.array([bank]))]}

    def ind(win, off, words=False):
        ap = win["ap"].bitcast(dt.uint32) if words else win["ap"]
        return {"ap": ap.indirect(off["ap"]), "acc": win["acc"], "off": off["acc"]}

    def order(q, key, reads, writes, chain=False):
        deps = set()
        for name, cols in reads:
            deps.update(int(i) for i in lastw[name][cols])
            if name == "ps":
                for k2, arr in lastr[name].items():
                    if k2 != key:
                        deps.update(int(i) for i in arr[cols])
        for name, cols in writes:
            if not chain:
                deps.update(int(i) for i in lastw[name][cols])
            for arr in lastr[name].values():
                deps.update(int(i) for i in arr[cols])
        deps.discard(-1)
        for i in sorted(deps, reverse=True):
            sem, cnt, clk = ops[i]
            if clock[q].get(sem, 0) < cnt:
                eng[q].wait_ge(T.sem[sem], cnt)
                for s2, c2 in clk.items():
                    if clock[q].get(s2, 0) < c2:
                        clock[q][s2] = c2

    def note(q, key, sem, inc, reads, writes):
        total[sem] = total.get(sem, 0) + inc
        clk = dict(clock[q]) if q else {}
        clk[sem] = total[sem]
        ops.append((sem, total[sem], clk))
        for name, cols in reads:
            if key not in lastr[name]:
                lastr[name][key] = np.full(width[name], -1)
            lastr[name][key][cols] = len(ops) - 1
        for name, cols in writes:
            lastw[name][cols] = len(ops) - 1

    def run(q, call, outs, ins, chain=False):
        reads, writes = [], []
        for d in ins:
            if isinstance(d, dict):
                reads += d["acc"] + d.get("off", [])
        for d in outs:
            writes += d["acc"]
            reads += d.get("off", [])
        order(q, q, reads, writes, chain)
        call().then_inc(T.sem[csem[q]], 1)
        note(q, q, csem[q], 1, reads, writes)

    def ap(d):
        return d["ap"] if isinstance(d, dict) else d

    def dmas(q, sem, pairs):
        reads, writes = [], []
        for o, i in pairs:
            writes += o["acc"]
            reads += i["acc"]
        order(q, sem, reads, writes)
        for o, i in pairs:
            eng[q].dma_start(o["ap"], i["ap"]).then_inc(T.sem[sem], 16)
        note(q, sem, sem, 16 * len(pairs), reads, writes)

    def hbm(a):
        return {"ap": a, "acc": []}

    def bytes_of(d):
        return {"ap": d["ap"].bitcast(dt.uint8), "acc": d["acc"]}

    def memset(o, c):
        run("v", lambda: g.vector.memset(o["ap"], c), [o], [])

    def copy(o, i):
        run("v", lambda: g.vector.tensor_copy(o["ap"], i["ap"]), [o], [i])

    def tten(o, a, b, op):
        run("v", lambda: g.vector.tensor_tensor(o["ap"], a["ap"], b["ap"], op), [o], [a, b])

    def tsc(o, a, s1, op0, s2=None, op1=None):
        if op1 is None:
            run("v", lambda: g.vector.tensor_scalar(o["ap"], a["ap"], ap(s1), None, op0), [o], [a, s1])
        else:
            run("v", lambda: g.vector.tensor_scalar(o["ap"], a["ap"], ap(s1), ap(s2), op0, op1), [o], [a, s1, s2])

    def scan(o, d0, d1, op0, op1, init=0.0):
        run("v", lambda: g.vector.tensor_tensor_scan(o["ap"], d0["ap"], d1["ap"], ap(init), op0, op1), [o], [d0, d1, init])

    def turn(o, i):
        run("v", lambda: g.vector.transpose(o["ap"], i["ap"]), [o], [i])

    def quant(qn, sn, a, n, tile):
        qo, so_ = S(qn, a, a + n), S(sn, a, a + n)
        run("v", lambda: g.vector.quantize_mx(qo["ap"], so_["ap"], tile["ap"]), [qo, so_], [tile])

    def act(o, i, func=AF.Copy, bias=None, scale=None, acc=None):
        kw = {}
        if bias is not None:
            kw["bias"] = ap(bias)
        if scale is not None:
            kw["scale"] = scale
        if acc is not None:
            kw["accum_out"] = acc["ap"]
        run("a", lambda: g.scalar.activation(o["ap"], i["ap"], func, **kw), [o] + ([acc] if acc else []), [i, bias])

    def mm(bank, lq, ls, la, rq, rs, ra, n, start=True, stop=True):
        o = P(bank, 0, n)
        a, b, c, d = S(lq, la, la + 128), S(ls, la, la + 128), S(rq, ra, ra + n), S(rs, ra, ra + n)
        run("p", lambda: g.tensor.matmul_mx(o["ap"], a["ap"], b["ap"], c["ap"], d["ap"], start, stop), [o], [a, b, c, d], chain=not start)

    def iota(o, pat, base, cm, small=False):
        if small:
            run("g", lambda: g.iota(o["ap"], pat, base, cm, allow_small_or_imprecise_dtypes=True), [o], [])
        else:
            run("g", lambda: g.iota(o["ap"], pat, base, cm), [o], [])

    def select(o, i, pat, op, fill, base, cm):
        run("g", lambda: g.affine_select(o["ap"], i["ap"], pat, op, fill, base, cm), [o], [i])

    def pick(qo, so_, off):
        src = ind(S("qu0"), off, True)
        run("v", lambda: g.vector.tensor_copy(qo["ap"].bitcast(dt.uint32), src["ap"]), [qo], [src])
        act(so_, ind(S("su0"), off))

    def engines(src, dst):
        e = topo.engines(src, dst)
        return sum(1 << k for k in e), len(e)

    def send(qn, sn, dst, rsem, lsem):
        rid, pid, _ = topo.addr(dst)
        mask, n = engines(core, dst)
        qi, si = S(qn, 64, 128), S(sn, 64, 128)
        order("g", lsem, qi["acc"] + si["acc"], [])
        g.remote_dma(T[qn][:, 128:192].bitcast(dt.uint8), qi["ap"].bitcast(dt.uint8), T.sem[rsem], T.sem[lsem], pid, rid, mask)
        g.remote_dma(T[sn][:, 128:192], si["ap"], T.sem[rsem], T.sem[lsem], pid, rid, mask)
        note("g", lsem, lsem, 2 * n, qi["acc"] + si["acc"], [])

    def arrives(qn, sn, src, rsem):
        note(None, rsem, rsem, 2 * engines(src, core)[1], [], S(qn, 128, 192)["acc"] + S(sn, 128, 192)["acc"])

    def slot(c, n):
        k, e = divmod(24 - c, 4)
        return S("bt", 4 * TO[k] + e, 4 * (TO[k] + n), 4)

    def col(name, j):
        return S(name, j, j + 1)

    def zero(o, n):
        act(o, S("ones", 0, n), scale=0.0)

    for t in range(3):
        arrives("qm%d" % t, "sm%d" % t, T.cores[(rank - STEP[t]) % n_ranks], "rm%d" % t)
        arrives("qz%d" % t, "sz%d" % t, T.cores[(rank + STEP[t]) % n_ranks], "rz%d" % t)

    dmas("s", "lu", [(S("ut"), hbm(T.u[:]))])
    dmas("a", "lh", [(S("x0", 4 * H, 4 * C), hbm(T.x[:, 4 * H:4 * C]))])
    dmas("s", "lx", [(S("x0", 0, 4 * H), hbm(T.x[:, 0:4 * H]))])
    order("s", "lx", S("x0")["acc"], [])
    dmas("s", "lw", [(bytes_of(S("wq")), hbm(T.wc[:])), (S("wsc"), hbm(T.ws[:]))])
    dmas("s", "lv", [(S("vt"), hbm(T.v[:]))])

    memset(S("ones"), 1.0)
    iota(S("ip", 0, 1), [[1, 1]], 0, 1)
    iota(S("uli", 0, 8), [[16, 8]], 0, 0)
    iota(S("xm"), [[0, 24], [1, 16]], 0, 0, True)
    select(S("comb"), S("ones"), [[1, 516]], A.is_equal, 0.0, -3, -4)
    select(S("g0"), S("ones", 0, 512), [[-16, 8], [0, 64]], A.is_ge, 0.0, 0, 1)
    select(S("gt"), S("g0"), [[16, 8], [0, 64]], A.is_ge, 0.0, 15, -1)
    iota(S("i2"), [[-16, 24], [1, 16]], 240, 0, True)
    iota(S("o0"), [[256, 2]], 0, 0, True)
    iota(S("vals"), [[1, 384]], -128, 0, True)
    iota(S("m0"), [[16, 24]], 0, 0, True)
    iota(S("ctab"), [[1, 64], [0, 6]], 0, 0, True)
    iota(S("uli", 8, 40), [[16, 4], [32, 4], [0, 2]], 112, 0)

    def padding(k):
        a, b = TO[k] + 16 * (21 - 4 * k), TO[k + 1] if k < 5 else TO[k] + TW[k]
        zero(S("bt", 4 * a, 4 * b), 4 * (b - a))

    for k in range(4):
        padding(k)
    memset(S("k1"), -BIG * 1024)
    for j, m in enumerate([31, 16, 15, 1]):
        tsc(col("ip", 1 + j), col("ip", 0), m, A.bitwise_and)
    memset(S("k1", 0, C, 16), BIG * 1024)
    memset(S("keep"), 1.0)
    copy(S("pf", 0, 5), S("ip", 0, 5))
    copy(S("ulg"), S("uli", 0, 8))
    memset(S("keep", 0, C, 16), 0.0)
    tsc(col("pf", 5), col("pf", 3), 16.0, A.mult, col("pf", 2), A.add)
    tsc(col("pf", 6), col("pf", 2), 4.0, A.mult)
    tsc(col("pf", 7), col("pf", 3), 2.5, A.subtract)
    tsc(col("pf", 8), col("pf", 4), 368.0, A.mult, col("pf", 5), A.add)
    tsc(col("pf", 9), col("pf", 2), 128.0, A.add)
    memset(S("k2"), -BIG)
    tsc(S("tbd"), S("xm"), col("pf", 3), A.not_equal, 2 * BIG, A.mult)
    memset(S("k2", 0, C, E), BIG)
    quant("qu0", "su0", 0, 128, S("ut"))
    pick(S("qug"), S("sug"), S("ulg"))
    for k in range(4, 6):
        padding(k)
    zero(col("racc", 0), 1)
    zero(S("mt", 0, 256), 256)
    zero(S("zt", 0, 256), 256)

    for t in range(3):
        first = t == 0
        qm, sm, qz, sz = "qm%d" % t, "sm%d" % t, "qz%d" % t, "sz%d" % t
        xs = "x0" if first else "xt"
        quant("qx", "sx", H, C - H, S(xs, 4 * H, 4 * C))
        mm(7, "qug", "sug", 0, "qx", "sx", H, C - H)
        quant("qx", "sx", 0, H, S(xs, 0, 4 * H))
        mm(4, "qug", "sug", 0, "qx", "sx", 0, H)
        mm(5, "qug", "sug", 0, "qx", "sx", 0, C)
        tten(S("md", H, C), P(7, 0, C - H), S("tbd", H, C), A.add)
        if first:
            quant("qe", "se", 0, 128, S("comb", 3, 515))
        scan(S("fill", H, C), S("k1", H, C), S("md", H, C), A.max, A.min)
        tten(S("md", 0, H), P(4, 0, H), S("tbd", 0, H), A.add)
        tten(S("bt", 4 * H, 4 * C, 4), P(7, 0, C - H), S("fill", H, C), A.is_gt)

        scan(S("fill", 0, H), S("k1", 0, H), S("md", 0, H), A.max, A.min)
        rows = list(range(23, NV, -1))
        for i in range(len(rows) + 1):
            if i < len(rows):
                c = rows[i]
                act(S("nu", 368 * (i % 3), 368 * (i % 3) + 16 * c), P(5, 0, 16 * c), AF.Sign, col("fill", 16 * c + 15), -1.0)
            if i > 0:
                c = rows[i - 1]
                k = (i - 1) % 3
                act(slot(c, 16 * c), S("nu", 368 * k, 368 * k + 16 * c), AF.Sign, 1.0, -1.0, col("racc", c))

        def row(c):
            tsc(slot(c, 16 * c), P(4, 0, 16 * c), col("fill", 16 * c + 15), A.is_ge)

        def inner(c):
            return 512 - 16 + 16 * c + 15

        def rowsum(c):
            scan(S("jr", 512 * (c + 1) - 16 * c, 512 * (c + 1)), slot(c, 16 * c), slot(c, 16 * c), A.add, A.max)

        low, high = [], []

        def sums(k):
            n = TW[k] + (64 if first and k == 3 else 0)
            quant("qb", "sb", TO[k], n, S("bt", 4 * TO[k], 4 * (TO[k] + n)))
            if k < 4:
                high.append(k)
                mm(6, "qg", "sg", 0, "qb", "sb", TO[k] + 128, max(128, TW[k] - 128), len(high) == 1, len(high) == 4)
            low.append(k)
            mm(7, "qg", "sg", 0, "qb", "sb", TO[k], 128, len(low) == 1, len(low) == 6)

        if first:
            for b in range(1, 4):
                quant("qe", "se", 128 * b, 128, S("comb", 3 - b, 515 - b))
        for b in range(4):
            mm(b, "qe", "se", 128 * b, "qx", "sx", 0, C)
        tten(slot(24, H), P(4, 0, H), S("fill", 0, H), A.is_gt)
        row(NV)
        scan(S("jr", inner(0) - 15, inner(0) - 15 + C), S("keep"), slot(24, C), A.mult, A.add)
        for c in range(NV - 1, 0, -1):
            row(c)
            if NS <= c + 1 <= NT:
                rowsum(c + 1)
            if first and c == 9:
                quant("qg", "sg", 0, 128, S("gt"))
                scan(S("tb2"), S("i2"), S("tbd"), A.min, A.add, BIG)
                tsc(S("ogu"), S("o0"), col("pf", 8), A.add, 767.0, A.min)
            for k in AFTER.get(c, []):
                sums(k)
        for c in list(range(NV, NT, -1)) + list(range(NS - 1, 0, -1)):
            act(S("junk", 256 * (c % 2), 256 * (c % 2) + 16 * c), slot(c, 16 * c), acc=col("racc", c))
        if first:
            zero(S("sw"), 416)
        for b in range(4):
            act(S("ts", C * b, C * b + C), P(b, 0, C), scale=-1.0)
        copy(S("racc", NS, NT + 1), S("jr", 512 * (NS + 1) - 1, 512 * (NT + 1), 512))
        tten(S("md2", 128, C), S("tb2", 128, C), P(6, 0, C - 128), A.subtract)
        tten(S("md2", 0, 128), S("tb2", 0, 128), P(7, 0, 128), A.subtract)
        scan(S("cs", 128, C), S("k1", 128, C), S("md2", 128, C), A.max, A.min)
        scan(S("cs", 0, 128), S("k1", 0, 128), S("md2", 0, 128), A.max, A.min)
        tten(S("pre"), S("jr", inner(0), inner(24), 16), S("racc"), A.add)
        tten(S("posf"), S("pre"), S("cs", 15, C, 16), A.add)
        tsc(S("posu"), S("posf"), col("pf", 9), A.add)
        copy(ind(S("sw", 0, 400), S("posu")), S("vals"))
        turn(S("tt", 0, C), S("sw", 0, C))
        turn(S("tt", C, 2 * C), S("sw", 16, 16 + C))
        tsc(S("ou"), ind(S("tt"), S("ogu")), 128.0, A.add)

        def win(b):
            return S("ts", C * b, C * b + C)

        def cells(b):
            scan(S("so", C * b, C * b + C), S("k2"), S("am", C * b, C * b + C), A.max, A.min)

        act(S("am", C, 2 * C), ind(win(1), S("ou", 0, 24)))
        act(S("am", 2 * C, 3 * C), ind(win(2), S("ou", 0, 24)))
        act(S("am", 3 * C + 16 * GV, 4 * C), ind(win(3), S("ou", GV, 24)))
        copy(S("am", 0, C), ind(win(0), S("ou", 0, 24)))
        copy(S("am", 3 * C, 3 * C + 16 * GV), ind(win(3), S("ou", 0, GV)))
        for b in range(4):
            cells(b)
        for b in range(3):
            act(S("mt", 256 + b, 512, 4), S("so", C * b + 5, C * b + C, E), scale=-1.0)
        tsc(S("mt", 259, 512, 4), S("so", 3 * C + 5, 4 * C, E), -1.0, A.mult)
        if first:
            tsc(S("m1"), S("m0"), col("pf", 7), A.add, 1.0 / E, A.mult)
        quant(qm, sm, 0, 128, S("mt"))
        send(qm, sm, T.cores[(rank + STEP[t]) % n_ranks], "rm%d" % t, "lm%d" % t)

        def dev(b):
            tten(S("dev", C * b, C * b + C), ind(S("so", C * b, C * b + C), S("mcu")), S("am", C * b, C * b + C), A.subtract)

        def swap(a, b, sem):
            pairs = []
            for gr in range(8):
                e = gr ^ 1 if t % 2 == 0 else (gr + 1 if gr % 2 else gr - 1) % 8
                pairs.append((S("dev", C * (4 + a), C * (4 + b), p=(16 * gr, 16 * gr + 16)), S("dev", C * a, C * b, p=(16 * e, 16 * e + 16))))
            dmas("s", sem + str(t), pairs)

        if first:
            tsc(S("m2"), S("m1"), WHOLE, A.add, WHOLE, A.subtract)
        tsc(S("rku"), S("posf"), 128.0, A.add)
        if first:
            tsc(S("mcu"), S("m2"), float(E), A.mult, E - 1.0, A.add)
        if t % 2:
            act(S("rr"), ind(S("ctab"), S("rku")), AF.Identity, col("pf", 6))
        else:
            act(S("rr"), ind(S("ctab"), S("rku")))
        dev(0)
        if not first:
            swap(0, 1, "dw")
        else:
            tsc(S("ulj"), S("uli", 8, 40), 127, A.bitwise_and)
        dev(1)
        if first:
            copy(S("ul4"), S("ulj"))
        dev(2)
        if first:
            pick(S("qu4"), S("su4"), S("ul4"))

        for b in range(4):
            mm(b, "wq", "wsc", 128 * b, qm, sm, 64, 128)
        for b in range(4):
            act(S("zt", 256 + b, 512, 4), P(b, 64, 128), scale=0.015625)
        quant(qz, sz, 0, 128, S("zt"))
        send(qz, sz, T.cores[(rank - STEP[t]) % n_ranks], "rz%d" % t, "lz%d" % t)

        dev(3)
        order("s", "dx", S("dev", 3 * C, 4 * C)["acc"], [])
        if first:
            swap(0, 1, "dw")
        swap(1, 3, "dx")
        swap(3, 4, "dy")
        turn(S("rt"), S("rr"))
        tsc(S("ce"), S("posf"), 125.5, A.add, 1.0 / E, A.mult)
        tsc(S("rk"), S("posf"), 128.0, A.add)
        tsc(S("blu"), S("rt", 0, C, 16), 0.0, A.add)
        tsc(S("cu"), S("ce"), WHOLE, A.add, WHOLE, A.subtract)
        if first:
            quant("qv", "sv", 0, 128, S("vt"))

        nf = 2 if t % 2 else 1
        for h in range(nf):
            lo = 2 * h if t % 2 else 1
            mm(4 + 2 * h, "qu4", "su4", 128 * lo, qz, sz, 64, 128)
            mm(5 + 2 * h, "qu4", "su4", 128 * lo + 128, qz, sz, 64, 128)
        for b in range(4):
            mm(b, "qe", "se", 128 * b, qz, sz, 64, 128)
        copy(S("va", 0, 64), P(4, 64, 128))
        if nf == 2:
            act(S("va", 64, 128), P(6, 64, 128))
        for h in range(nf):
            tten(S("fl", 64 * h, 64 * h + 64), S("va", 64 * h, 64 * h + 64), P(5 + 2 * h, 64, 128), A.is_lt)
        act(S("fr", 16 * FV, C), ind(S("fl", 0, 64 * nf), S("blu", FV, 24)), scale=1536.0)
        copy(S("pz", 0, 64), P(0, 64, 128))
        tsc(S("fr", 0, 16 * FV), ind(S("fl", 0, 64 * nf), S("blu", 0, FV)), 1536.0, A.mult)
        turn(S("ft"), S("fr"))
        copy(S("pz", 64, 128), P(1, 64, 128))
        tten(S("offf"), S("ft", 0, C, 16), S("rk"), A.add)
        copy(S("pz", 128, 192), P(2, 64, 128))
        copy(S("offu"), S("offf"))
        copy(S("pz", 192, 256), P(3, 64, 128))
        for lo, hi in ([(0, C)] if t < 2 else [(0, LAST), (LAST, C)]):
            for b in range(4):
                act(S("pc", C * b + lo, C * b + hi), ind(S("pz", 64 * b, 64 * b + 64), S("cu", lo // 16, hi // 16)))
                tten(S("xt", 4 * lo + b, 4 * hi, 4), ind(S("dev", C * b, C * b + 1920), S("offu", lo // 16, hi // 16)), S("pc", C * b + lo, C * b + hi), A.add)
            if t == 2:
                k = 0 if lo == 0 else 1
                quant("qx", "sx", lo, hi - lo, S("xt", 4 * lo, 4 * hi))
                mm(4 + k, "qv", "sv", 0, "qx", "sx", lo, hi - lo)
                dmas("s", "so%d" % (1 + k), [(hbm(T.oc[:, 4 * lo:4 * hi]), bytes_of(S("qx", lo, hi)))])

    act(S("ys", 0, LAST), P(4, 0, LAST))
    dmas("a", "so3", [(hbm(T.y[:, 0:LAST]), S("ys", 0, LAST))])
    copy(S("ys", LAST, C), P(5, 0, C - LAST))
    sc = [(hbm(T.osc[4 * k:4 * k + 4, :]), S("sx", p=(32 * k, 32 * k + 4))) for k in range(4)]
    dmas("a", "so4", sc[0:2])
    dmas("s", "so5", sc[2:4])
    dmas("a", "so6", [(hbm(T.y[:, LAST:C]), S("ys", LAST, C))])
    for sem, cnt in total.items():
        g.wait_ge(T.sem[sem], cnt)
